import numpy as np
import ml_dtypes


def mxq(x, axis, fmt="e4m3"):
    dtype, down = {"e4m3": (ml_dtypes.float8_e4m3fn, 7), "e5m2": (ml_dtypes.float8_e5m2, 14)}[fmt]
    v = np.moveaxis(np.asarray(x, np.float32).astype(ml_dtypes.bfloat16).astype(np.float64), axis, -1)
    blocks = v.reshape(v.shape[:-1] + (-1, 32))
    amax = np.abs(blocks).max(-1, keepdims=True)
    byte = np.maximum(np.where(amax > 0, np.frexp(amax)[1] - 1 + 127, 0) - down, 1)
    scale = np.exp2(byte - 127.0)
    codes = (blocks / scale).astype(np.float32).astype(dtype).astype(np.float64)
    return np.moveaxis((codes * scale).reshape(v.shape), -1, axis)


WIDE = False


def mx_kscale(k):
    if not WIDE:
        return np.ones(k)
    levels = np.array([10, -10, 5, -5, 0])
    if k % 512:
        return np.exp2(np.random.permutation(np.resize(levels, k // 32))).repeat(32)
    a = np.empty((k // 512, 16))
    for p in range(k // 512):
        a[p, :8] = np.random.permutation(np.resize(levels, 8))
        for g in range(8):
            far = levels[np.abs(levels - a[p, g]) >= 10]
            a[p, g + 8] = far[np.random.randint(len(far))]
    return np.exp2(a.ravel()).repeat(32)


def f64(x):
    return np.asarray(x).astype(np.float64)


def striped(idx):
    return np.tile(np.asarray(idx).reshape(-1, 16).T, (8, 1)).astype(np.uint16)


def unstriped(offs):
    return offs[:16].T.reshape(-1).astype(np.int64)


def striped8(idx):
    return np.asarray(idx).reshape(8, -1, 16).transpose(0, 2, 1).reshape(128, -1).astype(np.uint16)


def unstriped8(offs):
    return offs.reshape(8, 16, -1).transpose(0, 2, 1).reshape(8, -1).astype(np.int64)


def pick8(x, idx, run):
    r = np.arange(len(x))
    return x[r[:, None], idx[r % (8 * run) // run]]


E2M1 = np.array([0.0, 0.5, 1.0, 1.5, 2.0, 3.0, 4.0, 6.0, -0.0, -0.5, -1.0, -1.5, -2.0, -3.0, -4.0, -6.0])


def pack_weight(w, fmt):
    k, n = w.shape
    w = f64(np.asarray(w, np.float32).astype(ml_dtypes.bfloat16)).reshape(k // 32, 32, n)
    amax = np.abs(w).max(1)
    if fmt == "e4m3":
        byte = np.frexp(amax)[1] - 1 + 127 - 7
    else:
        mant, ex = np.frexp(amax / 6.0)
        byte = np.where(mant > 0.5, ex, ex - 1) + 127
    byte = np.clip(np.where(amax > 0, byte, 1), 1, 254)
    scaled = (w * np.exp2(127.0 - byte)[:, None, :]).reshape(k, n).astype(np.float32)
    by_word = np.ascontiguousarray(scaled.reshape(k // 512, 128, 4, n).transpose(0, 1, 3, 2))
    if fmt == "e4m3":
        words = by_word.astype(ml_dtypes.float8_e4m3fn).view(np.uint8)
    else:
        c = by_word.astype(ml_dtypes.float4_e2m1fn).view(np.uint8) & 0xF
        words = (c[..., 0::2] | (c[..., 1::2] << 4)).reshape(k // 512, 128, 2 * n)
    return np.ascontiguousarray(words), np.ascontiguousarray(byte.astype(np.uint8).reshape(k // 512, 16, n))


def unpack_weight(words, scales, fmt):
    g, _, n = scales.shape
    words = np.ascontiguousarray(words).reshape(g, 128, n, -1)
    if fmt == "e4m3":
        vals = words.view(ml_dtypes.float8_e4m3fn).astype(np.float64)
    else:
        nib = np.empty((g, 128, n, 4), np.uint8)
        nib[..., 0::2] = words & 0xF
        nib[..., 1::2] = words >> 4
        vals = E2M1[nib]
    vals = vals * np.repeat(np.exp2(scales.astype(np.float64) - 127.0), 8, axis=1)[..., None]
    return vals.transpose(0, 1, 3, 2).reshape(g * 512, n)


def sigmoid(v):
    return 1.0 / (1.0 + np.exp(-v))


def bf(x):
    return np.asarray(x, np.float32).astype(ml_dtypes.bfloat16)


def planes(Y):
    r, m = Y.shape
    b = f64(bf(Y)).reshape(r // 32, 32, m)
    amax = np.abs(b).max(1)
    byte = np.clip(np.where(amax > 0, np.frexp(amax)[1] - 1 + 127 - 7, 1), 1, 254)
    codes = (b * np.exp2(127.0 - byte)[:, None, :]).reshape(r, m).astype(np.float32).astype(ml_dtypes.float8_e4m3fn).view(np.uint8)
    words = codes.reshape(r // 512, 128, 4, m).transpose(0, 1, 3, 2)
    return np.ascontiguousarray(words), np.ascontiguousarray(byte.astype(np.uint8).reshape(r // 512, 16, m))


K, R, F, T, J, M = 512, 512, 512, 2048, 512, 128


def setup_inputs():
    n = np.random.standard_normal
    idx = np.random.permutation(T)[:J]
    idx2 = np.stack([np.random.permutation(J)[:M] for _ in range(8)])
    fk = mx_kscale(K)
    fr = mx_kscale(R)
    tabp = pack_weight(n((K, T)) / fk[:, None], "e2m1")
    dtabp = pack_weight(n((K, T)) / fk[:, None], "e2m1")
    return {
        "tab_words": tabp[0],
        "tab_scales": tabp[1],
        "dtab_words": dtabp[0],
        "dtab_scales": dtabp[1],
        "w1": (n((K, R)) * 1 / np.sqrt(K) * fk[:, None]).astype(np.float32),
        "bias": (np.random.uniform(-0.5, 0.5, (R, 1))).astype(np.float32),
        "gain": (np.random.uniform(0.5, 1.5, (R, 1))).astype(np.float32),
        "pw": (np.random.uniform(0.5, 1.5, (1, M))).astype(np.float32),
        "rs": (np.random.uniform(0.5, 2.0, (R, 1)) * fr[:, None]).astype(np.float32),
        "wor": (n((R, F)) * 1 / np.sqrt(R) / fr[:, None]).astype(np.float32),
        "res": (n((F, M)) * 0.5).astype(np.float32),
        "offs": striped(idx),
        "offs2": striped8(idx2),
    }


def reference(tab_words, tab_scales, dtab_words, dtab_scales, w1, bias, gain, pw, rs, wor, res, offs, offs2):
    idx = unstriped(offs)
    idx2 = unstriped8(offs2)
    tabu = unpack_weight(tab_words, tab_scales, "e2m1")
    dtabu = unpack_weight(dtab_words, dtab_scales, "e2m1")
    w1q = mxq(f64(w1), 0, "e4m3")
    tabidxg = tabu[:, idx]
    a = w1q.T @ tabidxg
    dtabidxg = dtabu[:, idx]
    ta = w1q.T @ dtabidxg
    h1 = np.tanh(a + f64(bias))
    h2 = h1 * f64(gain)
    s = pick8(h2, idx2, 64) * f64(pw)
    th1 = ta * (1.0 - np.square(h1))
    th2 = th1 * f64(gain)
    ts = pick8(th2, idx2, 64) * f64(pw)
    tu1 = ts * sigmoid(s) * (1.0 + s * (1.0 - sigmoid(s)))
    fo1 = tu1 * f64(rs)
    worq = mxq(f64(wor), 0, "e4m3")
    fo1q = mxq(fo1, 0, "e4m3")
    yo = worq.T @ fo1q
    y = yo + f64(res)
    words, scales = planes(y)
    return y, words, scales

@@ -1,0 +1,227 @@
+from contextlib import ExitStack
+
+import concourse.mybir as mybir
+
+F32 = mybir.dt.float32
+BF16 = mybir.dt.bfloat16
+I32 = mybir.dt.int32
+U32 = mybir.dt.uint32
+U16 = mybir.dt.uint16
+U8 = mybir.dt.uint8
+FP8X4 = mybir.dt.float8_e4m3fn_x4
+FP4X4 = mybir.dt.float4_e2m1fn_x4
+ACT = mybir.ActivationFunctionType
+ALU = mybir.AluOpType
+
+P = 128
+PACK = 4
+K, R, F, T, J, M = 512, 512, 512, 2048, 512, 128
+HALF = 256
+SCALAR_SHARE = 24
+FLOPS = 2 * (2 * K * R * J + R * F * M)
+
+
+def tile_attend_tcpick_o_pl_kernel(tc, tab_words, tab_scales, dtab_words, dtab_scales, w1, bias, gain, pw, rs, wor, res,
+                                    offs, offs2, out_0, out_1, out_2):
+    nc = tc.nc
+    with ExitStack() as ctx:
+        keep = ctx.enter_context(tc.tile_pool(name="keep", bufs=1))
+        psum = ctx.enter_context(tc.psum_pool(name="psum", bufs=1))
+
+        def sb(name, shape, dtype):
+            return keep.tile(shape, dtype, name=name, align_bytes=64)
+
+        slots = keep.tile([P, J // 16], U16, name="slots")
+        picks = keep.tile([P, M // 16], U16, name="picks")
+        tab_w = sb("tab_w", [P, T], U16)
+        tab_s = sb("tab_s", [P, T], U8)
+        dtab_w = sb("dtab_w", [P, T], U16)
+        dtab_s = sb("dtab_s", [P, T], U8)
+        w1_raw = [sb("w1_raw%d" % h, [P, PACK, HALF], F32) for h in range(2)]
+        wo_raw = [sb("wo_raw%d" % h, [P, PACK, HALF], F32) for h in range(2)]
+        bias_t = sb("bias_t", [P, PACK], F32)
+        gain_t = sb("gain_t", [P, PACK], F32)
+        rs_t = sb("rs_t", [P, PACK], F32)
+        pw_t = sb("pw_t", [P, M], F32)
+        res_t = sb("res_t", [P, PACK * M], F32)
+        zero = sb("zero", [P, 1], F32)
+        zero_b = sb("zero_b", [P, 1], F32)
+
+        def load_scale_rows(queue, plane, rows):
+            for q in range(4):
+                queue.dma_start(out=plane[32 * q:32 * q + 4, :].bitcast(I32), in_=rows[0, 4 * q:4 * q + 4, :].bitcast(I32))
+
+        def rows4(x):
+            return x.rearrange("(p j) c -> p j c", j=PACK)
+
+        nc.vector.memset(tab_s[:].bitcast(I32), 0)
+        nc.gpsimd.memset(dtab_s[:].bitcast(I32), 0)
+        nc.vector.memset(zero[:], 0.0)
+        nc.scalar.activation(zero_b[:], zero[:], ACT.Tanh)
+
+        nc.sync.dma_start(slots[:], offs)
+        nc.sync.dma_start(out=w1_raw[0][:], in_=rows4(w1)[:, :, 0:HALF])
+        load_scale_rows(nc.sync, tab_s, tab_scales)
+        nc.sync.dma_start(out=tab_w[:].bitcast(I32), in_=tab_words[0].bitcast(I32))
+        nc.sync.dma_start(out=w1_raw[1][:], in_=rows4(w1)[:, :, HALF:])
+        load_scale_rows(nc.sync, dtab_s, dtab_scales)
+        nc.sync.dma_start(out=bias_t[:], in_=bias.rearrange("(p t) o -> p (t o)", t=PACK))
+        nc.sync.dma_start(out=dtab_w[:].bitcast(I32), in_=dtab_words[0].bitcast(I32))
+        nc.sync.dma_start(out=gain_t[:], in_=gain.rearrange("(p t) o -> p (t o)", t=PACK))
+        nc.sync.dma_start(picks[:], offs2)
+        nc.sync.dma_start(out=pw_t[:], in_=pw[0].partition_broadcast(P))
+        nc.sync.dma_start(out=rs_t[:], in_=rs.rearrange("(p t) o -> p (t o)", t=PACK))
+        for h in range(2):
+            nc.sync.dma_start(out=wo_raw[h][:], in_=rows4(wor)[:, :, h * HALF:(h + 1) * HALF])
+        nc.sync.dma_start(out=res_t[:], in_=res.rearrange("(p t) m -> p (t m)", t=PACK))
+
+        def deal(copy, dst, raw, h, c0=0, c1=HALF // PACK):
+            first = h * (HALF // PACK)
+            copy(out=dst[:].rearrange("p (t c j) -> p c j t", t=PACK, j=PACK)[:, first + c0:first + c1],
+                 in_=raw[:].rearrange("p j (c t) -> p c j t", t=PACK)[:, c0:c1])
+
+        w1_bf = sb("w1_bf", [P, PACK * R], BF16)
+        w1_q = sb("w1_q", [P, R], U32)
+        w1_s = sb("w1_s", [P, R], U8)
+        tab_gw = sb("tab_gw", [P, J], U16)
+        tab_gs = sb("tab_gs", [P, J], U8)
+        dtab_gw = sb("dtab_gw", [P, J], U16)
+        dtab_gs = sb("dtab_gs", [P, J], U8)
+
+        deal(nc.scalar.copy, w1_bf, w1_raw[0], 0)
+        deal(nc.scalar.copy, w1_bf, w1_raw[1], 1, 0, SCALAR_SHARE)
+        nc.vector.tensor_copy(tab_gs[:], tab_s[:].indirect(slots[:]))
+        nc.vector.tensor_copy(tab_gw[:], tab_w[:].indirect(slots[:]))
+        deal(nc.vector.tensor_copy, w1_bf, w1_raw[1], 1, SCALAR_SHARE)
+        for t in range(PACK):
+            nc.vector.quantize_mx(out=w1_q[:, t * P:(t + 1) * P].bitcast(FP8X4), scales=w1_s[:, t * P:(t + 1) * P],
+                                  in_=w1_bf[:, t * PACK * P:(t + 1) * PACK * P])
+        nc.vector.tensor_copy(dtab_gs[:], dtab_s[:].indirect(slots[:]))
+        nc.vector.tensor_copy(dtab_gw[:], dtab_w[:].indirect(slots[:]))
+
+        nbias = sb("nbias", [P, PACK], F32)
+        ngain = sb("ngain", [P, PACK], F32)
+        pwrs = sb("pwrs", [P, PACK, M], F32)
+        nc.gpsimd.tensor_scalar(nbias[:], bias_t[:], -1.0, 0.0, ALU.mult, ALU.add)
+        nc.gpsimd.tensor_scalar(ngain[:], gain_t[:], -1.0, 0.0, ALU.mult, ALU.add)
+        for t in range(PACK):
+            nc.gpsimd.tensor_scalar(pwrs[:, t, :], pw_t[:], rs_t[:, t:t + 1], -0.25, ALU.mult, ALU.mult)
+
+        a_ps = [psum.tile([P, J], F32, name="bank_a%d" % t) for t in range(PACK)]
+        ta_ps = [psum.tile([P, J], F32, name="bank_t%d" % t) for t in range(PACK)]
+        for bank, words, scales in ((a_ps, tab_gw, tab_gs), (ta_ps, dtab_gw, dtab_gs)):
+            for t in range(PACK):
+                nc.tensor.matmul_mx(bank[t][:], lhsT=w1_q[:, t * P:(t + 1) * P].bitcast(FP8X4),
+                                    lhsT_scale=w1_s[:, t * P:(t + 1) * P],
+                                    rhs=words[:].bitcast(FP4X4), rhs_scale=scales[:], start=True, stop=True)
+
+        s = sb("s", [P, PACK, M], F32)
+        tn = sb("tn", [P, PACK, M], F32)
+        q1 = sb("q1", [P, PACK, M], F32)
+        u1 = sb("u1", [P, PACK, M], F32)
+        wt = sb("wt", [P, PACK, M], F32)
+        fo = sb("fo", [P, PACK, M], F32)
+        wo_bf = sb("wo_bf", [P, PACK * F], BF16)
+        wo_q = sb("wo_q", [P, F], U32)
+        wo_s = sb("wo_s", [P, F], U8)
+        h1n = [sb("h1n%d" % t, [P, J], F32) for t in range(PACK)]
+        h2 = [sb("h2_%d" % t, [P, J], F32) for t in range(PACK)]
+        part = [sb("part%d" % t, [P, J], F32) for t in range(PACK)]
+        th2 = [sb("th2_%d" % t, [P, J], F32) for t in range(PACK)]
+
+        def forward(t):
+            nc.scalar.activation(h1n[t][:], a_ps[t][:], ACT.Tanh, bias=nbias[:, t:t + 1], scale=-1.0)
+            nc.scalar.activation(h2[t][:], h1n[t][:], ACT.Copy, scale=ngain[:, t:t + 1])
+
+        def slope_on_scalar(t):
+            sq = sb("sq%d" % t, [P, J], F32)
+            nc.scalar.activation(sq[:], h1n[t][:], ACT.Square)
+            nc.scalar.activation(part[t][:], sq[:], ACT.Identity, bias=gain_t[:, t:t + 1], scale=ngain[:, t:t + 1])
+
+        def first_factor(t):
+            nc.vector.scalar_tensor_tensor(part[t][:], h1n[t][:], 1.0, ta_ps[t][:], ALU.add, ALU.mult)
+
+        def second_factor(t):
+            nc.vector.scalar_tensor_tensor(th2[t][:], h2[t][:], gain_t[:, t:t + 1], part[t][:], ALU.add, ALU.mult)
+
+        def times_slope(t):
+            nc.vector.tensor_tensor(th2[t][:], part[t][:], ta_ps[t][:], ALU.mult)
+
+        def pick_h2(t):
+            nc.vector.tensor_tensor(s[:, t, :], h2[t][:].indirect(picks[:]), pw_t[:], ALU.mult)
+
+        def pick_th2(t):
+            nc.vector.tensor_tensor(fo[:, t, :], th2[t][:].indirect(picks[:]), wt[:, t, :], ALU.mult)
+
+        def silu_tanh(ts):
+            nc.scalar.activation(tn[:, ts, :], s[:, ts, :], ACT.Tanh, bias=zero_b[:], scale=-0.5)
+
+        def silu_factors(ts):
+            nc.vector.scalar_tensor_tensor(q1[:, ts, :], tn[:, ts, :], 1.0, s[:, ts, :], ALU.add, ALU.mult)
+            nc.vector.scalar_tensor_tensor(u1[:, ts, :], tn[:, ts, :], -1.0, pwrs[:, ts, :], ALU.add, ALU.mult)
+
+        def silu_weight(ts):
+            nc.vector.scalar_tensor_tensor(wt[:, ts, :], q1[:, ts, :], 2.0, u1[:, ts, :], ALU.add, ALU.mult)
+
+        lo, hi = slice(0, 2), slice(2, 4)
+        forward(0)
+        forward(1)
+        forward(2)
+        pick_h2(0)
+        first_factor(0)
+        pick_h2(1)
+        silu_tanh(lo)
+        slope_on_scalar(2)
+        forward(3)
+        second_factor(0)
+        first_factor(1)
+        pick_h2(2)
+        second_factor(1)
+        times_slope(2)
+        silu_factors(lo)
+        pick_h2(3)
+        deal(nc.scalar.copy, wo_bf, wo_raw[0], 0)
+        silu_tanh(hi)
+        deal(nc.scalar.copy, wo_bf, wo_raw[1], 1)
+        silu_weight(lo)
+        first_factor(3)
+        pick_th2(0)
+        pick_th2(1)
+        second_factor(3)
+        silu_factors(hi)
+        nc.vector.quantize_mx(out=wo_q[:].bitcast(FP8X4), scales=wo_s[:], in_=wo_bf[:])
+        silu_weight(hi)
+        pick_th2(2)
+        pick_th2(3)
+
+        def weave(dst, src, m0, m1):
+            nc.vector.tensor_copy(dst[:].rearrange("p (c i t) -> p c t i", i=4, t=PACK)[:, m0 // 4:m1 // 4],
+                                  src[:].rearrange("p t (c i) -> p c t i", i=4)[:, m0 // 4:m1 // 4])
+
+        fo_bf = sb("fo_bf", [P, M * PACK], BF16)
+        fo_q = sb("fo_q", [P, M], U32)
+        fo_s = sb("fo_s", [P, M], U8)
+        weave(fo_bf, fo, 0, M)
+        nc.vector.quantize_mx(out=fo_q[:].bitcast(FP8X4), scales=fo_s[:], in_=fo_bf[:])
+
+        yo = psum.tile([P, PACK, M], F32, name="bank_a0")
+        for t in range(PACK):
+            nc.tensor.matmul_mx(yo[:, t, :], lhsT=wo_q[:, t * P:(t + 1) * P].bitcast(FP8X4),
+                                lhsT_scale=wo_s[:, t * P:(t + 1) * P],
+                                rhs=fo_q[:].bitcast(FP8X4), rhs_scale=fo_s[:], start=True, stop=True)
+        y = sb("y", [P, PACK, M], F32)
+        y_bf = sb("y_bf", [P, M * PACK], BF16)
+        y_q = sb("y_q", [P, M], U32)
+        y_s = sb("y_s", [P, M], U8)
+        res3 = res_t[:].rearrange("p (t m) -> p t m", t=PACK)
+        for m0 in (0, M // 2):
+            cols = slice(m0, m0 + M // 2)
+            nc.vector.tensor_tensor(y[:, :, cols], yo[:, :, cols], res3[:, :, cols], ALU.add)
+        nc.sync.dma_start(out=out_0.rearrange("(p t) m -> p t m", t=PACK), in_=y[:])
+        for m0 in (0, M // 2):
+            weave(y_bf, y, m0, m0 + M // 2)
+        nc.vector.quantize_mx(out=y_q[:].bitcast(FP8X4), scales=y_s[:], in_=y_bf[:])
+        nc.sync.dma_start(out=out_1[0].rearrange("p c t -> p (c t)").bitcast(I32), in_=y_q[:].bitcast(I32))
+        for q in range(4):
+            queue = nc.scalar if q % 2 == 0 else nc.sync
+            queue.dma_start(out=out_2[0, 4 * q:4 * q + 4, :].bitcast(I32), in_=y_s[32 * q:32 * q + 4, :].bitcast(I32))

@@ -1,6 +1,7 @@
 from contextlib import ExitStack
 
 import concourse.mybir as mybir
+from concourse.masks import make_identity
 
 F32 = mybir.dt.float32
 BF16 = mybir.dt.bfloat16
@@ -16,8 +17,6 @@ ALU = mybir.AluOpType
 P = 128
 PACK = 4
 K, R, F, T, J, M = 512, 512, 512, 2048, 512, 128
-HALF = 256
-SCALAR_SHARE = 24
 FLOPS = 2 * (2 * K * R * J + R * F * M)
 
 
@@ -28,8 +27,8 @@ def tile_attend_tcpick_o_pl_kernel(tc, tab_words, tab_scales, dtab_words, dtab_s
         keep = ctx.enter_context(tc.tile_pool(name="keep", bufs=1))
         psum = ctx.enter_context(tc.psum_pool(name="psum", bufs=1))
 
-        def sb(name, shape, dtype):
-            return keep.tile(shape, dtype, name=name, align_bytes=64)
+        def sb(name, shape, dtype, tag=None):
+            return keep.tile(shape, dtype, name=name, tag=tag or name, align_bytes=64)
 
         slots = keep.tile([P, J // 16], U16, name="slots")
         picks = keep.tile([P, M // 16], U16, name="picks")
@@ -37,8 +36,10 @@ def tile_attend_tcpick_o_pl_kernel(tc, tab_words, tab_scales, dtab_words, dtab_s
         tab_s = sb("tab_s", [P, T], U8)
         dtab_w = sb("dtab_w", [P, T], U16)
         dtab_s = sb("dtab_s", [P, T], U8)
-        w1_raw = [sb("w1_raw%d" % h, [P, PACK, HALF], F32) for h in range(2)]
-        wo_raw = [sb("wo_raw%d" % h, [P, PACK, HALF], F32) for h in range(2)]
+        w1_raw = [sb("w1_raw%d" % h, [P, PACK, R // 2], F32) for h in range(2)]
+        wo_raw = sb("wo_raw", [P, PACK, F], F32)
+        pw_col = sb("pw_col", [P, 1], F32)
+        ident = sb("ident", [P, P], F32)
         bias_t = sb("bias_t", [P, PACK], F32)
         gain_t = sb("gain_t", [P, PACK], F32)
         rs_t = sb("rs_t", [P, PACK], F32)
@@ -48,37 +49,49 @@ def tile_attend_tcpick_o_pl_kernel(tc, tab_words, tab_scales, dtab_words, dtab_s
         zero_b = sb("zero_b", [P, 1], F32)
 
         def load_scale_rows(queue, plane, rows):
-            for q in range(4):
-                queue.dma_start(out=plane[32 * q:32 * q + 4, :].bitcast(I32), in_=rows[0, 4 * q:4 * q + 4, :].bitcast(I32))
+            for i in range(4):
+                queue.dma_start(out=plane[i:P:32, :].bitcast(I32), in_=rows[0, i:16:4, :].bitcast(I32))
 
         def rows4(x):
             return x.rearrange("(p j) c -> p j c", j=PACK)
 
         nc.vector.memset(tab_s[:].bitcast(I32), 0)
-        nc.gpsimd.memset(dtab_s[:].bitcast(I32), 0)
+        nc.vector.memset(dtab_s[:].bitcast(I32), 0)
         nc.vector.memset(zero[:], 0.0)
-        nc.scalar.activation(zero_b[:], zero[:], ACT.Tanh)
+        make_identity(nc, ident[:])
 
+        nc.scalar.activation(zero_b[:], zero[:], ACT.Silu)
+
+        with nc.allow_non_contiguous_dma(reason="one weight a partition"):
+            nc.scalar.dma_start(out=pw_col[:], in_=pw.rearrange("o m -> m o"))
+        nc.scalar.dma_start(out=rs_t[:], in_=rs.rearrange("(p t) o -> p (t o)", t=PACK))
         nc.sync.dma_start(slots[:], offs)
-        nc.sync.dma_start(out=w1_raw[0][:], in_=rows4(w1)[:, :, 0:HALF])
-        load_scale_rows(nc.sync, tab_s, tab_scales)
         nc.sync.dma_start(out=tab_w[:].bitcast(I32), in_=tab_words[0].bitcast(I32))
-        nc.sync.dma_start(out=w1_raw[1][:], in_=rows4(w1)[:, :, HALF:])
+        load_scale_rows(nc.sync, tab_s, tab_scales)
+        for h in range(2):
+            nc.sync.dma_start(out=w1_raw[h][:], in_=rows4(w1)[:, :, h * (R // 2):(h + 1) * (R // 2)])
         load_scale_rows(nc.sync, dtab_s, dtab_scales)
         nc.sync.dma_start(out=bias_t[:], in_=bias.rearrange("(p t) o -> p (t o)", t=PACK))
         nc.sync.dma_start(out=dtab_w[:].bitcast(I32), in_=dtab_words[0].bitcast(I32))
         nc.sync.dma_start(out=gain_t[:], in_=gain.rearrange("(p t) o -> p (t o)", t=PACK))
         nc.sync.dma_start(picks[:], offs2)
-        nc.sync.dma_start(out=pw_t[:], in_=pw[0].partition_broadcast(P))
-        nc.sync.dma_start(out=rs_t[:], in_=rs.rearrange("(p t) o -> p (t o)", t=PACK))
-        for h in range(2):
-            nc.sync.dma_start(out=wo_raw[h][:], in_=rows4(wor)[:, :, h * HALF:(h + 1) * HALF])
+        nc.sync.dma_start(out=wo_raw[:], in_=rows4(wor))
         nc.sync.dma_start(out=res_t[:], in_=res.rearrange("(p t) m -> p (t m)", t=PACK))
 
-        def deal(copy, dst, raw, h, c0=0, c1=HALF // PACK):
-            first = h * (HALF // PACK)
-            copy(out=dst[:].rearrange("p (t c j) -> p c j t", t=PACK, j=PACK)[:, first + c0:first + c1],
-                 in_=raw[:].rearrange("p j (c t) -> p c j t", t=PACK)[:, c0:c1])
+        rs_q = sb("rs_q", [P, PACK], F32)
+        pwrs = sb("pwrs", [P, PACK, M], F32)
+        pw_ps = psum.tile([P, M], F32, name="bank_t3")
+        nc.tensor.transpose(pw_ps[:], pw_col[:].to_broadcast([P, P]), ident[:])
+        nc.scalar.mul(rs_q[:], rs_t[:], 0.5)
+        nc.scalar.copy(pw_t[:], pw_ps[:])
+        for t in range(PACK):
+            nc.scalar.activation(pwrs[:, t, :], pw_ps[:], ACT.Copy, scale=rs_q[:, t:t + 1])
+
+        def deal(copy, dst, raw, ts, cs=slice(0, P)):
+            copy(out=dst.rearrange("p (t c j) -> p c j t", t=2, j=PACK)[:, cs],
+                 in_=raw[:].rearrange("p j (c t) -> p c j t", t=PACK)[:, :, :, ts])
+
+        lo, hi = slice(0, 2), slice(2, 4)
 
         w1_bf = sb("w1_bf", [P, PACK * R], BF16)
         w1_q = sb("w1_q", [P, R], U32)
@@ -88,24 +101,27 @@ def tile_attend_tcpick_o_pl_kernel(tc, tab_words, tab_scales, dtab_words, dtab_s
         dtab_gw = sb("dtab_gw", [P, J], U16)
         dtab_gs = sb("dtab_gs", [P, J], U8)
 
-        deal(nc.scalar.copy, w1_bf, w1_raw[0], 0)
-        deal(nc.scalar.copy, w1_bf, w1_raw[1], 1, 0, SCALAR_SHARE)
-        nc.vector.tensor_copy(tab_gs[:], tab_s[:].indirect(slots[:]))
+        def quantise(q, sc, bf, t0, t1):
+            nc.vector.quantize_mx(out=q[:, t0 * P:t1 * P].bitcast(FP8X4), scales=sc[:, t0 * P:t1 * P],
+                                  in_=bf)
+
+        left, right = slice(0, P // 2), slice(P // 2, P)
+        deal(nc.scalar.copy, w1_bf[:, :1024], w1_raw[0], lo, left)
+        deal(nc.scalar.copy, w1_bf[:, 1024:], w1_raw[0], hi, left)
+        deal(nc.scalar.copy, w1_bf[:, 1024:], w1_raw[1], hi, right)
         nc.vector.tensor_copy(tab_gw[:], tab_w[:].indirect(slots[:]))
-        deal(nc.vector.tensor_copy, w1_bf, w1_raw[1], 1, SCALAR_SHARE)
-        for t in range(PACK):
-            nc.vector.quantize_mx(out=w1_q[:, t * P:(t + 1) * P].bitcast(FP8X4), scales=w1_s[:, t * P:(t + 1) * P],
-                                  in_=w1_bf[:, t * PACK * P:(t + 1) * PACK * P])
+        nc.vector.tensor_copy(tab_gs[:], tab_s[:].indirect(slots[:]))
+        deal(nc.vector.tensor_copy, w1_bf[:, :1024], w1_raw[1], lo, right)
+        quantise(w1_q, w1_s, w1_bf[:, :512], 0, 1)
+        quantise(w1_q, w1_s, w1_bf[:, 512:1024], 1, 2)
+        quantise(w1_q, w1_s, w1_bf[:, 1024:], 2, 4)
         nc.vector.tensor_copy(dtab_gs[:], dtab_s[:].indirect(slots[:]))
         nc.vector.tensor_copy(dtab_gw[:], dtab_w[:].indirect(slots[:]))
 
         nbias = sb("nbias", [P, PACK], F32)
         ngain = sb("ngain", [P, PACK], F32)
-        pwrs = sb("pwrs", [P, PACK, M], F32)
-        nc.gpsimd.tensor_scalar(nbias[:], bias_t[:], -1.0, 0.0, ALU.mult, ALU.add)
-        nc.gpsimd.tensor_scalar(ngain[:], gain_t[:], -1.0, 0.0, ALU.mult, ALU.add)
-        for t in range(PACK):
-            nc.gpsimd.tensor_scalar(pwrs[:, t, :], pw_t[:], rs_t[:, t:t + 1], -0.25, ALU.mult, ALU.mult)
+        nc.scalar.mul(nbias[:], bias_t[:], -1.0)
+        nc.scalar.mul(ngain[:], gain_t[:], -1.0)
 
         a_ps = [psum.tile([P, J], F32, name="bank_a%d" % t) for t in range(PACK)]
         ta_ps = [psum.tile([P, J], F32, name="bank_t%d" % t) for t in range(PACK)]
@@ -115,13 +131,11 @@ def tile_attend_tcpick_o_pl_kernel(tc, tab_words, tab_scales, dtab_words, dtab_s
                                     lhsT_scale=w1_s[:, t * P:(t + 1) * P],
                                     rhs=words[:].bitcast(FP4X4), rhs_scale=scales[:], start=True, stop=True)
 
-        s = sb("s", [P, PACK, M], F32)
+        s = sb("s", [P, PACK, M], F32, "dtab_w")
         tn = sb("tn", [P, PACK, M], F32)
         q1 = sb("q1", [P, PACK, M], F32)
         u1 = sb("u1", [P, PACK, M], F32)
         wt = sb("wt", [P, PACK, M], F32)
-        fo = sb("fo", [P, PACK, M], F32)
-        wo_bf = sb("wo_bf", [P, PACK * F], BF16)
         wo_q = sb("wo_q", [P, F], U32)
         wo_s = sb("wo_s", [P, F], U8)
         h1n = [sb("h1n%d" % t, [P, J], F32) for t in range(PACK)]
@@ -155,41 +169,43 @@ def tile_attend_tcpick_o_pl_kernel(tc, tab_words, tab_scales, dtab_words, dtab_s
 
         def silu_tanh(ts):
             nc.scalar.activation(tn[:, ts, :], s[:, ts, :], ACT.Tanh, bias=zero_b[:], scale=-0.5)
+            nc.scalar.activation(q1[:, ts, :], s[:, ts, :], ACT.Silu, bias=zero_b[:], scale=-1.0)
 
         def silu_factors(ts):
-            nc.vector.scalar_tensor_tensor(q1[:, ts, :], tn[:, ts, :], 1.0, s[:, ts, :], ALU.add, ALU.mult)
             nc.vector.scalar_tensor_tensor(u1[:, ts, :], tn[:, ts, :], -1.0, pwrs[:, ts, :], ALU.add, ALU.mult)
 
         def silu_weight(ts):
-            nc.vector.scalar_tensor_tensor(wt[:, ts, :], q1[:, ts, :], 2.0, u1[:, ts, :], ALU.add, ALU.mult)
+            nc.vector.scalar_tensor_tensor(wt[:, ts, :], q1[:, ts, :], -1.0, u1[:, ts, :], ALU.add, ALU.mult)
 
-        lo, hi = slice(0, 2), slice(2, 4)
         forward(0)
         forward(1)
-        forward(2)
         pick_h2(0)
-        first_factor(0)
         pick_h2(1)
+        forward(2)
         silu_tanh(lo)
         slope_on_scalar(2)
         forward(3)
-        second_factor(0)
+        first_factor(0)
         first_factor(1)
-        pick_h2(2)
+        second_factor(0)
         second_factor(1)
-        times_slope(2)
+        pick_h2(2)
         silu_factors(lo)
-        pick_h2(3)
-        deal(nc.scalar.copy, wo_bf, wo_raw[0], 0)
-        silu_tanh(hi)
-        deal(nc.scalar.copy, wo_bf, wo_raw[1], 1)
+        times_slope(2)
         silu_weight(lo)
+        pick_h2(3)
+        silu_tanh(hi)
         first_factor(3)
+        second_factor(3)
+        fo = sb("fo", [P, PACK, M], F32, "h2_3")
+        wo_lo = sb("wo_lo", [P, 2 * F], BF16, "h1n2")
+        wo_hi = sb("wo_hi", [P, 2 * F], BF16, "dtab_w")
+        deal(nc.scalar.copy, wo_lo[:], wo_raw, lo)
+        deal(nc.scalar.copy, wo_hi[:], wo_raw, hi)
         pick_th2(0)
         pick_th2(1)
-        second_factor(3)
         silu_factors(hi)
-        nc.vector.quantize_mx(out=wo_q[:].bitcast(FP8X4), scales=wo_s[:], in_=wo_bf[:])
+        quantise(wo_q, wo_s, wo_lo[:], 0, 2)
         silu_weight(hi)
         pick_th2(2)
         pick_th2(3)
@@ -202,11 +218,12 @@ def tile_attend_tcpick_o_pl_kernel(tc, tab_words, tab_scales, dtab_words, dtab_s
         fo_q = sb("fo_q", [P, M], U32)
         fo_s = sb("fo_s", [P, M], U8)
         weave(fo_bf, fo, 0, M)
+        quantise(wo_q, wo_s, wo_hi[:], 2, 4)
         nc.vector.quantize_mx(out=fo_q[:].bitcast(FP8X4), scales=fo_s[:], in_=fo_bf[:])
 
-        yo = psum.tile([P, PACK, M], F32, name="bank_a0")
+        yo = [psum.tile([P, 2, M], F32, name="bank_a%d" % h) for h in range(2)]
         for t in range(PACK):
-            nc.tensor.matmul_mx(yo[:, t, :], lhsT=wo_q[:, t * P:(t + 1) * P].bitcast(FP8X4),
+            nc.tensor.matmul_mx(yo[t // 2][:, t % 2, :], lhsT=wo_q[:, t * P:(t + 1) * P].bitcast(FP8X4),
                                 lhsT_scale=wo_s[:, t * P:(t + 1) * P],
                                 rhs=fo_q[:].bitcast(FP8X4), rhs_scale=fo_s[:], start=True, stop=True)
         y = sb("y", [P, PACK, M], F32)
@@ -214,14 +231,15 @@ def tile_attend_tcpick_o_pl_kernel(tc, tab_words, tab_scales, dtab_words, dtab_s
         y_q = sb("y_q", [P, M], U32)
         y_s = sb("y_s", [P, M], U8)
         res3 = res_t[:].rearrange("p (t m) -> p t m", t=PACK)
+        nc.vector.tensor_tensor(y[:, lo, :], yo[0][:], res3[:, lo, :], ALU.add)
         for m0 in (0, M // 2):
             cols = slice(m0, m0 + M // 2)
-            nc.vector.tensor_tensor(y[:, :, cols], yo[:, :, cols], res3[:, :, cols], ALU.add)
+            nc.vector.tensor_tensor(y[:, hi, cols], yo[1][:, :, cols], res3[:, hi, cols], ALU.add)
         nc.sync.dma_start(out=out_0.rearrange("(p t) m -> p t m", t=PACK), in_=y[:])
         for m0 in (0, M // 2):
             weave(y_bf, y, m0, m0 + M // 2)
         nc.vector.quantize_mx(out=y_q[:].bitcast(FP8X4), scales=y_s[:], in_=y_bf[:])
         nc.sync.dma_start(out=out_1[0].rearrange("p c t -> p (c t)").bitcast(I32), in_=y_q[:].bitcast(I32))
-        for q in range(4):
-            queue = nc.scalar if q % 2 == 0 else nc.sync
-            queue.dma_start(out=out_2[0, 4 * q:4 * q + 4, :].bitcast(I32), in_=y_s[32 * q:32 * q + 4, :].bitcast(I32))
+        for i in range(4):
+            queue = nc.scalar if i % 2 == 0 else nc.sync
+            queue.dma_start(out=out_2[0, i:16:4, :].bitcast(I32), in_=y_s[i:P:32, :].bitcast(I32))

@@ -177,38 +177,39 @@ def tile_attend_tcpick_o_pl_kernel(tc, tab_words, tab_scales, dtab_words, dtab_s
         def silu_weight(ts):
             nc.vector.scalar_tensor_tensor(wt[:, ts, :], q1[:, ts, :], -1.0, u1[:, ts, :], ALU.add, ALU.mult)
 
+        early, last = slice(0, 3), slice(3, 4)
         forward(0)
         forward(1)
         pick_h2(0)
         pick_h2(1)
+        slope_on_scalar(0)
         forward(2)
-        silu_tanh(lo)
-        slope_on_scalar(2)
-        forward(3)
-        first_factor(0)
-        first_factor(1)
-        second_factor(0)
-        second_factor(1)
+        first_factor(2)
+        times_slope(0)
         pick_h2(2)
-        silu_factors(lo)
-        times_slope(2)
-        silu_weight(lo)
-        pick_h2(3)
-        silu_tanh(hi)
+        second_factor(2)
+        forward(3)
+        silu_tanh(early)
+        slope_on_scalar(1)
         first_factor(3)
+        pick_h2(3)
+        silu_factors(early)
         second_factor(3)
+        silu_weight(early)
+        silu_tanh(last)
         fo = sb("fo", [P, PACK, M], F32, "h2_3")
-        wo_lo = sb("wo_lo", [P, 2 * F], BF16, "h1n2")
-        wo_hi = sb("wo_hi", [P, 2 * F], BF16, "dtab_w")
+        wo_lo = sb("wo_lo", [P, 2 * F], BF16, "dtab_w")
+        wo_hi = sb("wo_hi", [P, 2 * F], BF16, "sq1")
         deal(nc.scalar.copy, wo_lo[:], wo_raw, lo)
         deal(nc.scalar.copy, wo_hi[:], wo_raw, hi)
         pick_th2(0)
-        pick_th2(1)
-        silu_factors(hi)
-        quantise(wo_q, wo_s, wo_lo[:], 0, 2)
-        silu_weight(hi)
+        times_slope(1)
+        silu_factors(last)
         pick_th2(2)
+        silu_weight(last)
+        pick_th2(1)
         pick_th2(3)
+        quantise(wo_q, wo_s, wo_hi[:], 2, 4)
 
         def weave(dst, src, m0, m1):
             nc.vector.tensor_copy(dst[:].rearrange("p (c i t) -> p c t i", i=4, t=PACK)[:, m0 // 4:m1 // 4],
@@ -218,7 +219,7 @@ def tile_attend_tcpick_o_pl_kernel(tc, tab_words, tab_scales, dtab_words, dtab_s
         fo_q = sb("fo_q", [P, M], U32)
         fo_s = sb("fo_s", [P, M], U8)
         weave(fo_bf, fo, 0, M)
-        quantise(wo_q, wo_s, wo_hi[:], 2, 4)
+        quantise(wo_q, wo_s, wo_lo[:], 0, 2)
         nc.vector.quantize_mx(out=fo_q[:].bitcast(FP8X4), scales=fo_s[:], in_=fo_bf[:])
 
         yo = [psum.tile([P, 2, M], F32, name="bank_a%d" % h) for h in range(2)]

from contextlib import ExitStack

import concourse.mybir as mybir
from concourse.masks import make_identity

F32 = mybir.dt.float32
BF16 = mybir.dt.bfloat16
I32 = mybir.dt.int32
U32 = mybir.dt.uint32
U16 = mybir.dt.uint16
U8 = mybir.dt.uint8
FP8X4 = mybir.dt.float8_e4m3fn_x4
FP4X4 = mybir.dt.float4_e2m1fn_x4
ACT = mybir.ActivationFunctionType
ALU = mybir.AluOpType

P = 128
PACK = 4
K, R, F, T, J, M = 512, 512, 512, 2048, 512, 128
FLOPS = 2 * (2 * K * R * J + R * F * M)


def tile_attend_tcpick_o_pl_kernel(tc, tab_words, tab_scales, dtab_words, dtab_scales, w1, bias, gain, pw, rs, wor, res,
                                    offs, offs2, out_0, out_1, out_2):
    nc = tc.nc
    with ExitStack() as ctx:
        keep = ctx.enter_context(tc.tile_pool(name="keep", bufs=1))
        psum = ctx.enter_context(tc.psum_pool(name="psum", bufs=1))

        def sb(name, shape, dtype, tag=None):
            return keep.tile(shape, dtype, name=name, tag=tag or name, align_bytes=64)

        slots = keep.tile([P, J // 16], U16, name="slots")
        picks = keep.tile([P, M // 16], U16, name="picks")
        tab_w = sb("tab_w", [P, T], U16)
        tab_s = sb("tab_s", [P, T], U8)
        dtab_w = sb("dtab_w", [P, T], U16)
        dtab_s = sb("dtab_s", [P, T], U8)
        w1_raw = [sb("w1_raw%d" % h, [P, PACK, R // 2], F32) for h in range(2)]
        wo_raw = sb("wo_raw", [P, PACK, F], F32)
        pw_col = sb("pw_col", [P, 1], F32)
        ident = sb("ident", [P, P], F32)
        bias_t = sb("bias_t", [P, PACK], F32)
        gain_t = sb("gain_t", [P, PACK], F32)
        rs_t = sb("rs_t", [P, PACK], F32)
        pw_t = sb("pw_t", [P, M], F32)
        res_t = sb("res_t", [P, PACK * M], F32)
        zero = sb("zero", [P, 1], F32)
        zero_b = sb("zero_b", [P, 1], F32)

        def load_scale_rows(queue, plane, rows):
            for i in range(4):
                queue.dma_start(out=plane[i:P:32, :].bitcast(I32), in_=rows[0, i:16:4, :].bitcast(I32))

        def rows4(x):
            return x.rearrange("(p j) c -> p j c", j=PACK)

        nc.vector.memset(tab_s[:].bitcast(I32), 0)
        nc.vector.memset(dtab_s[:].bitcast(I32), 0)
        nc.vector.memset(zero[:], 0.0)
        make_identity(nc, ident[:])

        nc.scalar.activation(zero_b[:], zero[:], ACT.Silu)

        with nc.allow_non_contiguous_dma(reason="one weight a partition"):
            nc.scalar.dma_start(out=pw_col[:], in_=pw.rearrange("o m -> m o"))
        nc.scalar.dma_start(out=rs_t[:], in_=rs.rearrange("(p t) o -> p (t o)", t=PACK))
        nc.sync.dma_start(slots[:], offs)
        nc.sync.dma_start(out=tab_w[:].bitcast(I32), in_=tab_words[0].bitcast(I32))
        load_scale_rows(nc.sync, tab_s, tab_scales)
        for h in range(2):
            nc.sync.dma_start(out=w1_raw[h][:], in_=rows4(w1)[:, :, h * (R // 2):(h + 1) * (R // 2)])
        load_scale_rows(nc.sync, dtab_s, dtab_scales)
        nc.sync.dma_start(out=bias_t[:], in_=bias.rearrange("(p t) o -> p (t o)", t=PACK))
        nc.sync.dma_start(out=dtab_w[:].bitcast(I32), in_=dtab_words[0].bitcast(I32))
        nc.sync.dma_start(out=gain_t[:], in_=gain.rearrange("(p t) o -> p (t o)", t=PACK))
        nc.sync.dma_start(picks[:], offs2)
        nc.sync.dma_start(out=wo_raw[:], in_=rows4(wor))
        nc.sync.dma_start(out=res_t[:], in_=res.rearrange("(p t) m -> p (t m)", t=PACK))

        rs_q = sb("rs_q", [P, PACK], F32)
        pwrs = sb("pwrs", [P, PACK, M], F32)
        pw_ps = psum.tile([P, M], F32, name="bank_t3")
        nc.tensor.transpose(pw_ps[:], pw_col[:].to_broadcast([P, P]), ident[:])
        nc.scalar.mul(rs_q[:], rs_t[:], 0.5)
        nc.scalar.copy(pw_t[:], pw_ps[:])
        for t in range(PACK):
            nc.scalar.activation(pwrs[:, t, :], pw_ps[:], ACT.Copy, scale=rs_q[:, t:t + 1])

        def deal(copy, dst, raw, ts, cs=slice(0, P)):
            copy(out=dst.rearrange("p (t c j) -> p c j t", t=2, j=PACK)[:, cs],
                 in_=raw[:].rearrange("p j (c t) -> p c j t", t=PACK)[:, :, :, ts])

        lo, hi = slice(0, 2), slice(2, 4)

        w1_bf = sb("w1_bf", [P, PACK * R], BF16)
        w1_q = sb("w1_q", [P, R], U32)
        w1_s = sb("w1_s", [P, R], U8)
        tab_gw = sb("tab_gw", [P, J], U16)
        tab_gs = sb("tab_gs", [P, J], U8)
        dtab_gw = sb("dtab_gw", [P, J], U16)
        dtab_gs = sb("dtab_gs", [P, J], U8)

        def quantise(q, sc, bf, t0, t1):
            nc.vector.quantize_mx(out=q[:, t0 * P:t1 * P].bitcast(FP8X4), scales=sc[:, t0 * P:t1 * P],
                                  in_=bf)

        left, right = slice(0, P // 2), slice(P // 2, P)
        deal(nc.scalar.copy, w1_bf[:, :1024], w1_raw[0], lo, left)
        deal(nc.scalar.copy, w1_bf[:, 1024:], w1_raw[0], hi, left)
        deal(nc.scalar.copy, w1_bf[:, 1024:], w1_raw[1], hi, right)
        nc.vector.tensor_copy(tab_gw[:], tab_w[:].indirect(slots[:]))
        nc.vector.tensor_copy(tab_gs[:], tab_s[:].indirect(slots[:]))
        deal(nc.vector.tensor_copy, w1_bf[:, :1024], w1_raw[1], lo, right)
        quantise(w1_q, w1_s, w1_bf[:, :512], 0, 1)
        quantise(w1_q, w1_s, w1_bf[:, 512:1024], 1, 2)
        quantise(w1_q, w1_s, w1_bf[:, 1024:], 2, 4)
        nc.vector.tensor_copy(dtab_gs[:], dtab_s[:].indirect(slots[:]))
        nc.vector.tensor_copy(dtab_gw[:], dtab_w[:].indirect(slots[:]))

        nbias = sb("nbias", [P, PACK], F32)
        ngain = sb("ngain", [P, PACK], F32)
        nc.scalar.mul(nbias[:], bias_t[:], -1.0)
        nc.scalar.mul(ngain[:], gain_t[:], -1.0)

        a_ps = [psum.tile([P, J], F32, name="bank_a%d" % t) for t in range(PACK)]
        ta_ps = [psum.tile([P, J], F32, name="bank_t%d" % t) for t in range(PACK)]
        for bank, words, scales in ((a_ps, tab_gw, tab_gs), (ta_ps, dtab_gw, dtab_gs)):
            for t in range(PACK):
                nc.tensor.matmul_mx(bank[t][:], lhsT=w1_q[:, t * P:(t + 1) * P].bitcast(FP8X4),
                                    lhsT_scale=w1_s[:, t * P:(t + 1) * P],
                                    rhs=words[:].bitcast(FP4X4), rhs_scale=scales[:], start=True, stop=True)

        s = sb("s", [P, PACK, M], F32, "dtab_w")
        tn = sb("tn", [P, PACK, M], F32)
        q1 = sb("q1", [P, PACK, M], F32)
        u1 = sb("u1", [P, PACK, M], F32)
        wt = sb("wt", [P, PACK, M], F32)
        wo_q = sb("wo_q", [P, F], U32)
        wo_s = sb("wo_s", [P, F], U8)
        h1n = [sb("h1n%d" % t, [P, J], F32) for t in range(PACK)]
        h2 = [sb("h2_%d" % t, [P, J], F32) for t in range(PACK)]
        part = [sb("part%d" % t, [P, J], F32) for t in range(PACK)]
        th2 = [sb("th2_%d" % t, [P, J], F32) for t in range(PACK)]

        def forward(t):
            nc.scalar.activation(h1n[t][:], a_ps[t][:], ACT.Tanh, bias=nbias[:, t:t + 1], scale=-1.0)
            nc.scalar.activation(h2[t][:], h1n[t][:], ACT.Copy, scale=ngain[:, t:t + 1])

        def slope_on_scalar(t):
            sq = sb("sq%d" % t, [P, J], F32)
            nc.scalar.activation(sq[:], h1n[t][:], ACT.Square)
            nc.scalar.activation(part[t][:], sq[:], ACT.Identity, bias=gain_t[:, t:t + 1], scale=ngain[:, t:t + 1])

        def first_factor(t):
            nc.vector.scalar_tensor_tensor(part[t][:], h1n[t][:], 1.0, ta_ps[t][:], ALU.add, ALU.mult)

        def second_factor(t):
            nc.vector.scalar_tensor_tensor(th2[t][:], h2[t][:], gain_t[:, t:t + 1], part[t][:], ALU.add, ALU.mult)

        def times_slope(t):
            nc.vector.tensor_tensor(th2[t][:], part[t][:], ta_ps[t][:], ALU.mult)

        def pick_h2(t):
            nc.vector.tensor_tensor(s[:, t, :], h2[t][:].indirect(picks[:]), pw_t[:], ALU.mult)

        def pick_th2(t):
            nc.vector.tensor_tensor(fo[:, t, :], th2[t][:].indirect(picks[:]), wt[:, t, :], ALU.mult)

        def silu_tanh(ts):
            nc.scalar.activation(tn[:, ts, :], s[:, ts, :], ACT.Tanh, bias=zero_b[:], scale=-0.5)
            nc.scalar.activation(q1[:, ts, :], s[:, ts, :], ACT.Silu, bias=zero_b[:], scale=-1.0)

        def silu_factors(ts):
            nc.vector.scalar_tensor_tensor(u1[:, ts, :], tn[:, ts, :], -1.0, pwrs[:, ts, :], ALU.add, ALU.mult)

        def silu_weight(ts):
            nc.vector.scalar_tensor_tensor(wt[:, ts, :], q1[:, ts, :], -1.0, u1[:, ts, :], ALU.add, ALU.mult)

        early, last = slice(0, 3), slice(3, 4)
        forward(0)
        forward(1)
        pick_h2(0)
        pick_h2(1)
        slope_on_scalar(0)
        forward(2)
        first_factor(2)
        times_slope(0)
        pick_h2(2)
        second_factor(2)
        forward(3)
        silu_tanh(early)
        slope_on_scalar(1)
        first_factor(3)
        pick_h2(3)
        silu_factors(early)
        second_factor(3)
        silu_weight(early)
        silu_tanh(last)
        fo = sb("fo", [P, PACK, M], F32, "h2_3")
        wo_lo = sb("wo_lo", [P, 2 * F], BF16, "dtab_w")
        wo_hi = sb("wo_hi", [P, 2 * F], BF16, "sq1")
        deal(nc.scalar.copy, wo_lo[:], wo_raw, lo)
        deal(nc.scalar.copy, wo_hi[:], wo_raw, hi)
        pick_th2(0)
        times_slope(1)
        silu_factors(last)
        pick_th2(2)
        silu_weight(last)
        pick_th2(1)
        pick_th2(3)
        quantise(wo_q, wo_s, wo_hi[:], 2, 4)

        def weave(dst, src, m0, m1):
            nc.vector.tensor_copy(dst[:].rearrange("p (c i t) -> p c t i", i=4, t=PACK)[:, m0 // 4:m1 // 4],
                                  src[:].rearrange("p t (c i) -> p c t i", i=4)[:, m0 // 4:m1 // 4])

        fo_bf = sb("fo_bf", [P, M * PACK], BF16)
        fo_q = sb("fo_q", [P, M], U32)
        fo_s = sb("fo_s", [P, M], U8)
        weave(fo_bf, fo, 0, M)
        quantise(wo_q, wo_s, wo_lo[:], 0, 2)
        nc.vector.quantize_mx(out=fo_q[:].bitcast(FP8X4), scales=fo_s[:], in_=fo_bf[:])

        yo = [psum.tile([P, 2, M], F32, name="bank_a%d" % h) for h in range(2)]
        for t in range(PACK):
            nc.tensor.matmul_mx(yo[t // 2][:, t % 2, :], lhsT=wo_q[:, t * P:(t + 1) * P].bitcast(FP8X4),
                                lhsT_scale=wo_s[:, t * P:(t + 1) * P],
                                rhs=fo_q[:].bitcast(FP8X4), rhs_scale=fo_s[:], start=True, stop=True)
        y = sb("y", [P, PACK, M], F32)
        y_bf = sb("y_bf", [P, M * PACK], BF16)
        y_q = sb("y_q", [P, M], U32)
        y_s = sb("y_s", [P, M], U8)
        res3 = res_t[:].rearrange("p (t m) -> p t m", t=PACK)
        nc.vector.tensor_tensor(y[:, lo, :], yo[0][:], res3[:, lo, :], ALU.add)
        for m0 in (0, M // 2):
            cols = slice(m0, m0 + M // 2)
            nc.vector.tensor_tensor(y[:, hi, cols], yo[1][:, :, cols], res3[:, hi, cols], ALU.add)
        nc.sync.dma_start(out=out_0.rearrange("(p t) m -> p t m", t=PACK), in_=y[:])
        for m0 in (0, M // 2):
            weave(y_bf, y, m0, m0 + M // 2)
        nc.vector.quantize_mx(out=y_q[:].bitcast(FP8X4), scales=y_s[:], in_=y_bf[:])
        nc.sync.dma_start(out=out_1[0].rearrange("p c t -> p (c t)").bitcast(I32), in_=y_q[:].bitcast(I32))
        for i in range(4):
            queue = nc.scalar if i % 2 == 0 else nc.sync
            queue.dma_start(out=out_2[0, i:16:4, :].bitcast(I32), in_=y_s[i:P:32, :].bitcast(I32))
